import numpy as np
import ml_dtypes


def mxq(x, axis, fmt="e4m3"):
    dtype, down = {"e4m3": (ml_dtypes.float8_e4m3fn, 7), "e5m2": (ml_dtypes.float8_e5m2, 14)}[fmt]
    v = np.moveaxis(np.asarray(x, np.float32).astype(ml_dtypes.bfloat16).astype(np.float64), axis, -1)
    blocks = v.reshape(v.shape[:-1] + (-1, 32))
    amax = np.abs(blocks).max(-1, keepdims=True)
    byte = np.maximum(np.where(amax > 0, np.frexp(amax)[1] - 1 + 127, 0) - down, 1)
    scale = np.exp2(byte - 127.0)
    codes = (blocks / scale).astype(np.float32).astype(dtype).astype(np.float64)
    return np.moveaxis((codes * scale).reshape(v.shape), -1, axis)


WIDE = False


def mx_kscale(k):
    if not WIDE:
        return np.ones(k)
    levels = np.array([10, -10, 5, -5, 0])
    if k % 512:
        return np.exp2(np.random.permutation(np.resize(levels, k // 32))).repeat(32)
    a = np.empty((k // 512, 16))
    for p in range(k // 512):
        a[p, :8] = np.random.permutation(np.resize(levels, 8))
        for g in range(8):
            far = levels[np.abs(levels - a[p, g]) >= 10]
            a[p, g + 8] = far[np.random.randint(len(far))]
    return np.exp2(a.ravel()).repeat(32)


def f64(x):
    return np.asarray(x).astype(np.float64)


def striped(idx):
    return np.tile(idx.reshape(-1, 16).T, (8, 1)).astype(np.uint16)


def unstriped(offs):
    return offs[:16].T.reshape(-1).astype(np.int64)


def striped8(idx):
    return np.concatenate([x.reshape(-1, 16).T for x in idx]).astype(np.uint16)


def runs(offs, k):
    lists = np.stack([offs[16 * r : 16 * r + 16].T.reshape(-1) for r in range(8)]).astype(np.int64)
    return lists[np.arange(k) % 512 // 64]


def pack_weight(w):
    k, n = w.shape
    w = f64(np.asarray(w, np.float32).astype(ml_dtypes.bfloat16)).reshape(k // 32, 32, n)
    amax = np.abs(w).max(1)
    byte = np.clip(np.where(amax > 0, np.frexp(amax)[1] - 1 + 127 - 7, 1), 1, 254)
    scaled = (w * np.exp2(127.0 - byte)[:, None, :]).reshape(k, n).astype(np.float32)
    words = np.ascontiguousarray(scaled.reshape(k // 512, 128, 4, n).transpose(0, 1, 3, 2)).astype(ml_dtypes.float8_e4m3fn).view(np.uint8)
    return words, np.ascontiguousarray(byte.astype(np.uint8).reshape(k // 512, 16, n))


def unpack_weight(words, scales):
    g, p, n, _ = words.shape
    vals = np.ascontiguousarray(words).view(ml_dtypes.float8_e4m3fn).astype(np.float64) * np.repeat(np.exp2(scales.astype(np.float64) - 127.0), 8, axis=1)[..., None]
    return vals.transpose(0, 1, 3, 2).reshape(g * 512, n)


def sigmoid(v):
    return 1.0 / (1.0 + np.exp(-np.maximum(v, -700.0)))


K, T, S, H, W, G = 512, 1024, 512, 512, 256, 2048


def setup_inputs():
    n = np.random.standard_normal
    s = mx_kscale(K)[:, None]
    packed_xT = pack_weight(n((K, T)) * s)
    packed_dT = pack_weight(n((K, G)) / s)
    return {
        "x_words": packed_xT[0],
        "x_scales": packed_xT[1],
        "w1": (n((K, H)) / np.sqrt(K) / s).astype(np.float32),
        "w2": (n((K, H)) / np.sqrt(K) / s).astype(np.float32),
        "gs": (np.random.uniform(0.5, 1.5, (K, 1)) * s).astype(np.float32),
        "d_words": packed_dT[0],
        "d_scales": packed_dT[1],
        "offs": striped(np.random.permutation(T)[:S]),
        "two": striped(np.random.permutation(T)[:S]),
        "n1": striped8(np.stack([np.random.permutation(S)[:W] for _ in range(8)])),
        "n2": striped8(np.stack([np.random.permutation(S)[:W] for _ in range(8)])),
        "k1": striped8(np.random.randint(0, G, (8, H))),
        "n3": striped8(np.stack([np.random.permutation(S) for _ in range(8)])),
    }


def reference(x_words, x_scales, w1, w2, gs, d_words, d_scales, offs, two, n1, n2, k1, n3):
    d_k1 = unpack_weight(d_words, d_scales)[np.arange(K)[:, None], runs(k1, K)]
    x_two = unpack_weight(x_words, x_scales)[:, unstriped(two)]
    d = mxq(f64(w2), 0, "e4m3").T @ x_two
    xq = unpack_weight(x_words, x_scales)[:, unstriped(offs)]
    y = mxq(f64(w1), 0, "e4m3").T @ xq
    ra = d[np.arange(H)[:, None], runs(n2, H)] - (0.5 * (y[np.arange(H)[:, None], runs(n1, H)]))
    ds = y.copy()
    ds[np.arange(H)[:, None], runs(n1, H)] = ra
    z = f64(gs) * ds
    h = 0.0625 * ((d_k1.T @ mxq(z, 0, "e4m3")))
    st = h * (sigmoid(h[np.arange(H)[:, None], runs(n3, H)]))
    return np.maximum(st, st[np.arange(H)[:, None], runs(n3, H)])

@@ -1,0 +1,202 @@
+from contextlib import ExitStack
+
+import concourse.mybir as mybir
+
+K, T, S, H, W, G = 512, 1024, 512, 512, 256, 2048
+FLOPS = 3 * 2 * K * H * S
+
+F32 = mybir.dt.float32
+BF16 = mybir.dt.bfloat16
+I32 = mybir.dt.int32
+U32 = mybir.dt.uint32
+U16 = mybir.dt.uint16
+U8 = mybir.dt.uint8
+FP8X4 = mybir.dt.float8_e4m3fn_x4
+ALU = mybir.AluOpType
+ACT = mybir.ActivationFunctionType
+
+P = 128
+PACK = 4
+HALF = 256
+CUT = 384
+
+
+def tile_picked_twqputbtwicp_none_p_kernel(tc, x_words, x_scales, w1, w2, gs, d_words, d_scales, offs, two, n1, n2, k1, n3, out):
+    nc = tc.nc
+    with ExitStack() as ctx:
+        keep = ctx.enter_context(tc.tile_pool(name="keep", bufs=1))
+        psum = ctx.enter_context(tc.psum_pool(name="psum", bufs=1))
+
+        def sb(name, cols, dtype, tag=None):
+            return keep.tile([P, cols], dtype, name=name, tag=tag or name, align_bytes=64)
+
+        def load_list(name, src):
+            tile = keep.tile([P, src.shape[1]], U16, name=name)
+            nc.sync.dma_start(tile[:], src)
+            return tile
+
+        def load_words(name, src, cols):
+            tile = sb(name, cols, U32)
+            nc.sync.dma_start(tile[:].bitcast(I32), src[0].rearrange("p c r -> p (c r)").bitcast(I32))
+            return tile
+
+        def load_weight_half(name, src, half):
+            tile = keep.tile([P, PACK, HALF], F32, name=name, tag=name, align_bytes=64)
+            nc.sync.dma_start(tile[:], src.rearrange("(p j) c -> p j c", j=PACK)[:, :, half * HALF : (half + 1) * HALF])
+            return tile
+
+        x_scale_table = sb("x_scale_table", T, U8)
+        d_scale_table = sb("d_scale_table", G, U8)
+        d_plane = sb("d_plane", H, U8)
+        warm = sb("warm", 2, F32)
+        nc.vector.memset(x_scale_table[:].bitcast(I32), 0)
+        nc.vector.memset(warm[:, 0:1], 0.0)
+        nc.vector.memset(d_scale_table[:].bitcast(I32), 0)
+        nc.vector.memset(d_plane[:].bitcast(I32), 0)
+
+        offs_l = load_list("offs_l", offs)
+        two_l = load_list("two_l", two)
+        x_table = load_words("x_table", x_words, T)
+        for q in range(4):
+            nc.scalar.dma_start(x_scale_table[32 * q : 32 * q + 4, :].bitcast(I32), x_scales[0, 4 * q : 4 * q + 4, :].bitcast(I32))
+        nc.scalar.activation(warm[:, 1:2], warm[:, 0:1], ACT.Sigmoid)
+        w1_raw = [load_weight_half(f"w1_raw{half}", w1, half) for half in range(2)]
+        k1_l = load_list("k1_l", k1)
+        nc.sync.dma_start(d_scale_table[0:P:8, :].bitcast(I32), d_scales[0].bitcast(I32))
+        w2_raw = [load_weight_half(f"w2_raw{half}", w2, half) for half in range(2)]
+        gain = sb("gain", PACK, F32)
+        nc.sync.dma_start(gain[:], gs.rearrange("(p t) o -> p (t o)", t=PACK))
+        n1_l = load_list("n1_l", n1)
+        n2_l = load_list("n2_l", n2)
+        d_table = load_words("d_table", d_words, G)
+        n3_l = load_list("n3_l", n3)
+
+        def gather(name, table, offsets, dtype, tag=None):
+            picked = sb(name, S, dtype, tag)
+            nc.vector.tensor_copy(picked[:], table[:].indirect(offsets[:]))
+            return picked
+
+        def interleave_weight(name, raw):
+            grouped = sb(name, PACK * H, BF16)
+            view = grouped[:].rearrange("p (t m j) -> p m j t", t=PACK, j=PACK)
+            for half in range(2):
+                nc.scalar.copy(view[:, 64 * half : 64 * (half + 1)], raw[half][:].rearrange("p j (m t) -> p m j t", t=PACK))
+            return grouped
+
+        def quantize_weight(name, grouped):
+            codes = sb(name + "_codes", H, U32)
+            plane = sb(name + "_plane", H, U8)
+            nc.vector.quantize_mx(out=codes[:].bitcast(FP8X4), scales=plane[:], in_=grouped[:])
+            return codes, plane
+
+        def product(bank, lhs, t, rhs, cols):
+            rows = slice(P * t, P * (t + 1))
+            nc.tensor.matmul_mx(out=bank[:, cols], lhsT=lhs[0][:, rows].bitcast(FP8X4), lhsT_scale=lhs[1][:, rows],
+                                rhs=rhs[0][:, cols].bitcast(FP8X4), rhs_scale=rhs[1][:, cols], start=True, stop=True)
+
+        xq_plane = gather("xq_plane", x_scale_table, offs_l, U8)
+        xt_plane = gather("xt_plane", x_scale_table, two_l, U8)
+        xq = (gather("xq_codes", x_table, offs_l, U32), xq_plane)
+        xt = (gather("xt_codes", x_table, two_l, U32), xt_plane)
+        w1_grouped = interleave_weight("w1_grouped", w1_raw)
+        w2_grouped = interleave_weight("w2_grouped", w2_raw)
+        w1q = quantize_weight("w1", w1_grouped)
+        d_bytes = gather("d_bytes", d_scale_table, k1_l, U8, tag="w1_raw1")
+        w2q = quantize_weight("w2", w2_grouped)
+        d_bytes_dealt = sb("d_bytes_dealt", H, U8)
+        nc.vector.tensor_copy(d_bytes_dealt[:].rearrange("p (t m) -> p m t", t=PACK), d_bytes[:].rearrange("p (m t) -> p m t", t=PACK))
+        for r in range(4):
+            nc.sync.dma_start(d_plane[r:P:32, :].bitcast(I32), d_bytes_dealt[8 * r : P : 32, :].bitcast(I32))
+
+        y_bank = [psum.tile([P, S], F32, name=f"y_bank{t}", tag=f"bank{t}") for t in range(PACK)]
+        d_bank = [psum.tile([P, S], F32, name=f"d_bank{t}", tag=f"bank{PACK + t}") for t in range(PACK)]
+        for t in range(PACK):
+            product(y_bank[t], w1q, t, xq, slice(0, S))
+        for t in range(PACK):
+            product(d_bank[t], w2q, t, xt, slice(0, S))
+
+        z_rows = [sb(f"z_rows{t}", S, F32) for t in range(PACK)]
+        d_rows = [sb(f"d_rows{t}", S, F32) for t in range(PACK)]
+        own = [sb(f"own{t}", W, F32) for t in range(PACK)]
+        met = [sb(f"met{t}", W, F32) for t in range(PACK)]
+        z_grouped = sb("z_grouped", PACK * S, BF16)
+        z_view = z_grouped[:].rearrange("p (c t) -> p c t", t=PACK)
+        halves = [slice(half * HALF, (half + 1) * HALF) for half in range(2)]
+
+        def leave(rows, bank, t, cols=slice(0, S)):
+            nc.scalar.activation(rows[t][:, cols], bank[t][:, cols], ACT.Copy, scale=gain[:, t : t + 1])
+
+        def leave_pair(first, second):
+            leave(*second, slice(0, CUT))
+            leave(*first)
+            leave(*second, slice(CUT, S))
+
+        def fetch_own(t):
+            nc.vector.tensor_scalar(own[t][:], z_rows[t][:].indirect(n1_l[:]), -0.5, 0.0, ALU.mult, ALU.add)
+
+        def fetch_met(t):
+            nc.vector.tensor_copy(met[t][:], d_rows[t][:].indirect(n2_l[:]))
+
+        def put(t):
+            nc.vector.tensor_tensor(z_rows[t][:].indirect(n1_l[:]), own[t][:], met[t][:], ALU.add)
+
+        leave(z_rows, y_bank, 0)
+        leave(z_rows, y_bank, 1)
+        leave_pair((d_rows, d_bank, 0), (z_rows, y_bank, 2))
+        leave_pair((d_rows, d_bank, 1), (z_rows, y_bank, 3))
+        leave_pair((d_rows, d_bank, 2), (d_rows, d_bank, 3))
+
+        fetch_own(0)
+        fetch_own(1)
+        for t in range(2):
+            fetch_met(t)
+            fetch_own(t + 2)
+            put(t)
+        fetch_met(2)
+        fetch_met(3)
+        put(2)
+        put(3)
+        for t in range(PACK):
+            for cols in halves:
+                nc.scalar.copy(z_view[:, cols, t], z_rows[t][:, cols])
+
+        d_codes = gather("d_codes", d_table, k1_l, U32, tag="d_rows3")
+        d_codes_dealt = sb("d_codes_dealt", H, U32)
+        nc.vector.tensor_copy(d_codes_dealt[:].rearrange("p (t m) -> p m t", t=PACK), d_codes[:].rearrange("p (m t) -> p m t", t=PACK))
+
+        z_codes = sb("z_codes", S, U32)
+        z_plane = sb("z_plane", S, U8)
+        for half, cols in enumerate(halves):
+            nc.vector.quantize_mx(out=z_codes[:, cols].bitcast(FP8X4), scales=z_plane[:, cols],
+                                  in_=z_grouped[:, PACK * half * HALF : PACK * (half + 1) * HALF])
+
+        h_bank = [[psum.tile([P, S], F32, name=f"h_bank{t}_{half}", tag=f"bank{PACK * half + t}") for half in range(2)] for t in range(PACK)]
+        for t in range(PACK):
+            for half, cols in enumerate(halves):
+                product(h_bank[t][half], (d_codes_dealt, d_plane), t, (z_codes, z_plane), cols)
+
+        h_rows = [sb(f"h_rows{t}", S, F32) for t in range(PACK)]
+        gates = [sb(f"gates{t}", S, F32) for t in range(PACK)]
+        st_rows = [sb(f"st_rows{t}", S, F32) for t in range(PACK)]
+        other = [sb(f"other{t}", S, F32) for t in range(PACK)]
+        result = [sb(f"result{t}", S, F32) for t in range(PACK)]
+        out_view = out.rearrange("(p t) c -> p t c", t=PACK)
+        n3_halves = [n3_l[:, half * HALF // 16 : (half + 1) * HALF // 16] for half in range(2)]
+
+        def gate(t):
+            for half, cols in enumerate(halves):
+                nc.scalar.activation(h_rows[t][:, cols], h_bank[t][half][:, cols], ACT.Copy, scale=0.0625)
+            for half, cols in enumerate(halves):
+                nc.scalar.activation(gates[t][:, cols], h_rows[t][:].indirect(n3_halves[half]), ACT.Sigmoid)
+            for cols in halves:
+                nc.vector.tensor_tensor(st_rows[t][:, cols], h_rows[t][:, cols], gates[t][:, cols], ALU.mult)
+
+        gate(0)
+        for t in range(PACK):
+            for half, cols in enumerate(halves):
+                nc.vector.tensor_copy(other[t][:, cols], st_rows[t][:].indirect(n3_halves[half]))
+            if t + 1 < PACK:
+                gate(t + 1)
+            for cols in halves:
+                nc.vector.tensor_tensor(result[t][:, cols], st_rows[t][:, cols], other[t][:, cols], ALU.max)
+                nc.sync.dma_start(out_view[:, t, cols], result[t][:, cols])

@@ -89,24 +89,30 @@ def tile_picked_twqputbtwicp_none_p_kernel(tc, x_words, x_scales, w1, w2, gs, d_
             nc.vector.quantize_mx(out=codes[:].bitcast(FP8X4), scales=plane[:], in_=grouped[:])
             return codes, plane
 
-        def product(bank, lhs, t, rhs, cols):
+        def product(bank, lhs, t, rhs, cols, first=0):
             rows = slice(P * t, P * (t + 1))
-            nc.tensor.matmul_mx(out=bank[:, cols], lhsT=lhs[0][:, rows].bitcast(FP8X4), lhsT_scale=lhs[1][:, rows],
+            nc.tensor.matmul_mx(out=bank[:, cols], lhsT=lhs[0][:, P * (t - first) : P * (t - first + 1)].bitcast(FP8X4), lhsT_scale=lhs[1][:, rows],
                                 rhs=rhs[0][:, cols].bitcast(FP8X4), rhs_scale=rhs[1][:, cols], start=True, stop=True)
 
         xq_plane = gather("xq_plane", x_scale_table, offs_l, U8)
         xt_plane = gather("xt_plane", x_scale_table, two_l, U8)
         xq = (gather("xq_codes", x_table, offs_l, U32), xq_plane)
         xt = (gather("xt_codes", x_table, two_l, U32), xt_plane)
+        def deal(name, picked, tiles, dtype, run, tag=None):
+            count = tiles.stop - tiles.start
+            dealt = sb(name, count * P, dtype, tag)
+            nc.vector.tensor_copy(dealt[:].rearrange("p (t c i) -> p c t i", t=count, i=run),
+                                  picked[:].rearrange("p (c i t) -> p c t i", t=PACK, i=run)[:, :, tiles, :])
+            return dealt
+
         w1_grouped = interleave_weight("w1_grouped", w1_raw)
         w2_grouped = interleave_weight("w2_grouped", w2_raw)
         w1q = quantize_weight("w1", w1_grouped)
         d_bytes = gather("d_bytes", d_scale_table, k1_l, U8, tag="w1_raw1")
-        w2q = quantize_weight("w2", w2_grouped)
-        d_bytes_dealt = sb("d_bytes_dealt", H, U8)
-        nc.vector.tensor_copy(d_bytes_dealt[:].rearrange("p (t m) -> p m t", t=PACK), d_bytes[:].rearrange("p (m t) -> p m t", t=PACK))
+        d_bytes_dealt = deal("d_bytes_dealt", d_bytes, slice(0, PACK), U8, 16)
         for r in range(4):
             nc.sync.dma_start(d_plane[r:P:32, :].bitcast(I32), d_bytes_dealt[8 * r : P : 32, :].bitcast(I32))
+        w2q = quantize_weight("w2", w2_grouped)
 
         y_bank = [psum.tile([P, S], F32, name=f"y_bank{t}", tag=f"bank{t}") for t in range(PACK)]
         d_bank = [psum.tile([P, S], F32, name=f"d_bank{t}", tag=f"bank{PACK + t}") for t in range(PACK)]
@@ -126,10 +132,12 @@ def tile_picked_twqputbtwicp_none_p_kernel(tc, x_words, x_scales, w1, w2, gs, d_
         def leave(rows, bank, t, cols=slice(0, S)):
             nc.scalar.activation(rows[t][:, cols], bank[t][:, cols], ACT.Copy, scale=gain[:, t : t + 1])
 
-        def leave_pair(first, second):
-            leave(*second, slice(0, CUT))
+        def leave_together(first, *others):
+            for other_rows in others:
+                leave(*other_rows, slice(0, CUT))
             leave(*first)
-            leave(*second, slice(CUT, S))
+            for other_rows in others:
+                leave(*other_rows, slice(CUT, S))
 
         def fetch_own(t):
             nc.vector.tensor_scalar(own[t][:], z_rows[t][:].indirect(n1_l[:]), -0.5, 0.0, ALU.mult, ALU.add)
@@ -140,63 +148,81 @@ def tile_picked_twqputbtwicp_none_p_kernel(tc, x_words, x_scales, w1, w2, gs, d_
         def put(t):
             nc.vector.tensor_tensor(z_rows[t][:].indirect(n1_l[:]), own[t][:], met[t][:], ALU.add)
 
-        leave(z_rows, y_bank, 0)
-        leave(z_rows, y_bank, 1)
-        leave_pair((d_rows, d_bank, 0), (z_rows, y_bank, 2))
-        leave_pair((d_rows, d_bank, 1), (z_rows, y_bank, 3))
-        leave_pair((d_rows, d_bank, 2), (d_rows, d_bank, 3))
+        for t in range(PACK - 1):
+            leave(z_rows, y_bank, t)
+        leave_together((d_rows, d_bank, 0), (z_rows, y_bank, 3))
+        leave_together((d_rows, d_bank, 1), (d_rows, d_bank, 2), (d_rows, d_bank, 3))
 
-        fetch_own(0)
-        fetch_own(1)
-        for t in range(2):
+        for t in range(PACK - 1):
+            fetch_own(t)
+        fetch_met(0)
+        fetch_own(3)
+        put(0)
+        for t in range(1, PACK):
             fetch_met(t)
-            fetch_own(t + 2)
+        for t in range(1, PACK):
             put(t)
-        fetch_met(2)
-        fetch_met(3)
-        put(2)
-        put(3)
         for t in range(PACK):
             for cols in halves:
                 nc.scalar.copy(z_view[:, cols, t], z_rows[t][:, cols])
 
         d_codes = gather("d_codes", d_table, k1_l, U32, tag="d_rows3")
-        d_codes_dealt = sb("d_codes_dealt", H, U32)
-        nc.vector.tensor_copy(d_codes_dealt[:].rearrange("p (t m) -> p m t", t=PACK), d_codes[:].rearrange("p (m t) -> p m t", t=PACK))
-
         z_codes = sb("z_codes", S, U32)
         z_plane = sb("z_plane", S, U8)
-        for half, cols in enumerate(halves):
+
+        def quantize_z(half):
+            cols = halves[half]
             nc.vector.quantize_mx(out=z_codes[:, cols].bitcast(FP8X4), scales=z_plane[:, cols],
-                                  in_=z_grouped[:, PACK * half * HALF : PACK * (half + 1) * HALF])
+                                  in_=z_grouped[:, PACK * cols.start : PACK * cols.stop])
 
-        h_bank = [[psum.tile([P, S], F32, name=f"h_bank{t}_{half}", tag=f"bank{PACK * half + t}") for half in range(2)] for t in range(PACK)]
-        for t in range(PACK):
-            for half, cols in enumerate(halves):
-                product(h_bank[t][half], (d_codes_dealt, d_plane), t, (z_codes, z_plane), cols)
+        quantize_z(0)
+        d_codes_first = deal("d_codes_first", d_codes, slice(0, 1), U32, 4)
+        quantize_z(1)
+        d_codes_rest = deal("d_codes_rest", d_codes, slice(1, PACK), U32, 4, tag="z_grouped")
+        zq = (z_codes, z_plane)
 
-        h_rows = [sb(f"h_rows{t}", S, F32) for t in range(PACK)]
         gates = [sb(f"gates{t}", S, F32) for t in range(PACK)]
         st_rows = [sb(f"st_rows{t}", S, F32) for t in range(PACK)]
         other = [sb(f"other{t}", S, F32) for t in range(PACK)]
-        result = [sb(f"result{t}", S, F32) for t in range(PACK)]
         out_view = out.rearrange("(p t) c -> p t c", t=PACK)
-        n3_halves = [n3_l[:, half * HALF // 16 : (half + 1) * HALF // 16] for half in range(2)]
+
+        def places(cols):
+            return n3_l[:, cols.start // 16 : cols.stop // 16]
+
+        h_rows = [sb(f"h_rows{t}", S, F32) for t in range(PACK)]
+
+        def make_h(t):
+            if t == 0:
+                pieces = [(psum.tile([P, S], F32, name=f"h_first{half}", tag=f"bank{half}"), cols) for half, cols in enumerate(halves)]
+                lhs, first = (d_codes_first, d_plane), 0
+            else:
+                pieces = [(psum.tile([P, S], F32, name=f"h_bank{t}", tag=f"bank{1 + t % 2}"), slice(0, S))]
+                lhs, first = (d_codes_rest, d_plane), 1
+            for bank, cols in pieces:
+                product(bank, lhs, t, zq, cols, first)
+                if t == 1:
+                    nc.vector.tensor_scalar_mul(h_rows[t][:, cols], bank[:, cols], 0.0625)
+                else:
+                    nc.scalar.activation(h_rows[t][:, cols], bank[:, cols], ACT.Copy, scale=0.0625)
+            return pieces
+
+        h_pieces = {t: make_h(t) for t in range(2)}
 
         def gate(t):
-            for half, cols in enumerate(halves):
-                nc.scalar.activation(h_rows[t][:, cols], h_bank[t][half][:, cols], ACT.Copy, scale=0.0625)
-            for half, cols in enumerate(halves):
-                nc.scalar.activation(gates[t][:, cols], h_rows[t][:].indirect(n3_halves[half]), ACT.Sigmoid)
+            pieces = h_pieces[t] if t < 2 else make_h(t)
             for cols in halves:
-                nc.vector.tensor_tensor(st_rows[t][:, cols], h_rows[t][:, cols], gates[t][:, cols], ALU.mult)
+                nc.scalar.activation(gates[t][:, cols], h_rows[t][:].indirect(places(cols)), ACT.Sigmoid)
+            for bank, cols in pieces:
+                nc.vector.scalar_tensor_tensor(st_rows[t][:, cols], bank[:, cols], 0.0625, gates[t][:, cols], ALU.mult, ALU.mult)
 
         gate(0)
         for t in range(PACK):
-            for half, cols in enumerate(halves):
-                nc.vector.tensor_copy(other[t][:, cols], st_rows[t][:].indirect(n3_halves[half]))
-            if t + 1 < PACK:
+            last = t + 1 == PACK
+            for cols in [halves[0], slice(256, 384), slice(384, 512)] if last else halves:
+                nc.vector.tensor_copy(other[t][:, cols], st_rows[t][:].indirect(places(cols)))
+            if not last:
                 gate(t + 1)
-            for cols in halves:
-                nc.vector.tensor_tensor(result[t][:, cols], st_rows[t][:, cols], other[t][:, cols], ALU.max)
-                nc.sync.dma_start(out_view[:, t, cols], result[t][:, cols])
+            result = sb(f"result{t}", S, F32, tag=f"h_rows{(t + 1) % PACK}")
+            for cols in [halves[0], slice(256, 384), slice(384, 512)] if last else [slice(0, S)]:
+                nc.vector.tensor_tensor(result[:, cols], st_rows[t][:, cols], other[t][:, cols], ALU.max)
+                nc.sync.dma_start(out_view[:, t, cols], result[:, cols])

from contextlib import ExitStack

import concourse.mybir as mybir

K, T, S, H, W, G = 512, 1024, 512, 512, 256, 2048
FLOPS = 3 * 2 * K * H * S

F32 = mybir.dt.float32
BF16 = mybir.dt.bfloat16
I32 = mybir.dt.int32
U32 = mybir.dt.uint32
U16 = mybir.dt.uint16
U8 = mybir.dt.uint8
FP8X4 = mybir.dt.float8_e4m3fn_x4
ALU = mybir.AluOpType
ACT = mybir.ActivationFunctionType

P = 128
PACK = 4
HALF = 256
CUT = 384


def tile_picked_twqputbtwicp_none_p_kernel(tc, x_words, x_scales, w1, w2, gs, d_words, d_scales, offs, two, n1, n2, k1, n3, out):
    nc = tc.nc
    with ExitStack() as ctx:
        keep = ctx.enter_context(tc.tile_pool(name="keep", bufs=1))
        psum = ctx.enter_context(tc.psum_pool(name="psum", bufs=1))

        def sb(name, cols, dtype, tag=None):
            return keep.tile([P, cols], dtype, name=name, tag=tag or name, align_bytes=64)

        def load_list(name, src):
            tile = keep.tile([P, src.shape[1]], U16, name=name)
            nc.sync.dma_start(tile[:], src)
            return tile

        def load_words(name, src, cols):
            tile = sb(name, cols, U32)
            nc.sync.dma_start(tile[:].bitcast(I32), src[0].rearrange("p c r -> p (c r)").bitcast(I32))
            return tile

        def load_weight_half(name, src, half):
            tile = keep.tile([P, PACK, HALF], F32, name=name, tag=name, align_bytes=64)
            nc.sync.dma_start(tile[:], src.rearrange("(p j) c -> p j c", j=PACK)[:, :, half * HALF : (half + 1) * HALF])
            return tile

        x_scale_table = sb("x_scale_table", T, U8)
        d_scale_table = sb("d_scale_table", G, U8)
        d_plane = sb("d_plane", H, U8)
        warm = sb("warm", 2, F32)
        nc.vector.memset(x_scale_table[:].bitcast(I32), 0)
        nc.vector.memset(warm[:, 0:1], 0.0)
        nc.vector.memset(d_scale_table[:].bitcast(I32), 0)
        nc.vector.memset(d_plane[:].bitcast(I32), 0)

        offs_l = load_list("offs_l", offs)
        two_l = load_list("two_l", two)
        x_table = load_words("x_table", x_words, T)
        for q in range(4):
            nc.scalar.dma_start(x_scale_table[32 * q : 32 * q + 4, :].bitcast(I32), x_scales[0, 4 * q : 4 * q + 4, :].bitcast(I32))
        nc.scalar.activation(warm[:, 1:2], warm[:, 0:1], ACT.Sigmoid)
        w1_raw = [load_weight_half(f"w1_raw{half}", w1, half) for half in range(2)]
        k1_l = load_list("k1_l", k1)
        nc.sync.dma_start(d_scale_table[0:P:8, :].bitcast(I32), d_scales[0].bitcast(I32))
        w2_raw = [load_weight_half(f"w2_raw{half}", w2, half) for half in range(2)]
        gain = sb("gain", PACK, F32)
        nc.sync.dma_start(gain[:], gs.rearrange("(p t) o -> p (t o)", t=PACK))
        n1_l = load_list("n1_l", n1)
        n2_l = load_list("n2_l", n2)
        d_table = load_words("d_table", d_words, G)
        n3_l = load_list("n3_l", n3)

        def gather(name, table, offsets, dtype, tag=None):
            picked = sb(name, S, dtype, tag)
            nc.vector.tensor_copy(picked[:], table[:].indirect(offsets[:]))
            return picked

        def interleave_weight(name, raw):
            grouped = sb(name, PACK * H, BF16)
            view = grouped[:].rearrange("p (t m j) -> p m j t", t=PACK, j=PACK)
            for half in range(2):
                nc.scalar.copy(view[:, 64 * half : 64 * (half + 1)], raw[half][:].rearrange("p j (m t) -> p m j t", t=PACK))
            return grouped

        def quantize_weight(name, grouped):
            codes = sb(name + "_codes", H, U32)
            plane = sb(name + "_plane", H, U8)
            nc.vector.quantize_mx(out=codes[:].bitcast(FP8X4), scales=plane[:], in_=grouped[:])
            return codes, plane

        def product(bank, lhs, t, rhs, cols, first=0):
            rows = slice(P * t, P * (t + 1))
            nc.tensor.matmul_mx(out=bank[:, cols], lhsT=lhs[0][:, P * (t - first) : P * (t - first + 1)].bitcast(FP8X4), lhsT_scale=lhs[1][:, rows],
                                rhs=rhs[0][:, cols].bitcast(FP8X4), rhs_scale=rhs[1][:, cols], start=True, stop=True)

        xq_plane = gather("xq_plane", x_scale_table, offs_l, U8)
        xt_plane = gather("xt_plane", x_scale_table, two_l, U8)
        xq = (gather("xq_codes", x_table, offs_l, U32), xq_plane)
        xt = (gather("xt_codes", x_table, two_l, U32), xt_plane)
        def deal(name, picked, tiles, dtype, run, tag=None):
            count = tiles.stop - tiles.start
            dealt = sb(name, count * P, dtype, tag)
            nc.vector.tensor_copy(dealt[:].rearrange("p (t c i) -> p c t i", t=count, i=run),
                                  picked[:].rearrange("p (c i t) -> p c t i", t=PACK, i=run)[:, :, tiles, :])
            return dealt

        w1_grouped = interleave_weight("w1_grouped", w1_raw)
        w2_grouped = interleave_weight("w2_grouped", w2_raw)
        w1q = quantize_weight("w1", w1_grouped)
        d_bytes = gather("d_bytes", d_scale_table, k1_l, U8, tag="w1_raw1")
        d_bytes_dealt = deal("d_bytes_dealt", d_bytes, slice(0, PACK), U8, 16)
        for r in range(4):
            nc.sync.dma_start(d_plane[r:P:32, :].bitcast(I32), d_bytes_dealt[8 * r : P : 32, :].bitcast(I32))
        w2q = quantize_weight("w2", w2_grouped)

        y_bank = [psum.tile([P, S], F32, name=f"y_bank{t}", tag=f"bank{t}") for t in range(PACK)]
        d_bank = [psum.tile([P, S], F32, name=f"d_bank{t}", tag=f"bank{PACK + t}") for t in range(PACK)]
        for t in range(PACK):
            product(y_bank[t], w1q, t, xq, slice(0, S))
        for t in range(PACK):
            product(d_bank[t], w2q, t, xt, slice(0, S))

        z_rows = [sb(f"z_rows{t}", S, F32) for t in range(PACK)]
        d_rows = [sb(f"d_rows{t}", S, F32) for t in range(PACK)]
        own = [sb(f"own{t}", W, F32) for t in range(PACK)]
        met = [sb(f"met{t}", W, F32) for t in range(PACK)]
        z_grouped = sb("z_grouped", PACK * S, BF16)
        z_view = z_grouped[:].rearrange("p (c t) -> p c t", t=PACK)
        halves = [slice(half * HALF, (half + 1) * HALF) for half in range(2)]

        def leave(rows, bank, t, cols=slice(0, S)):
            nc.scalar.activation(rows[t][:, cols], bank[t][:, cols], ACT.Copy, scale=gain[:, t : t + 1])

        def leave_together(first, *others):
            for other_rows in others:
                leave(*other_rows, slice(0, CUT))
            leave(*first)
            for other_rows in others:
                leave(*other_rows, slice(CUT, S))

        def fetch_own(t):
            nc.vector.tensor_scalar(own[t][:], z_rows[t][:].indirect(n1_l[:]), -0.5, 0.0, ALU.mult, ALU.add)

        def fetch_met(t):
            nc.vector.tensor_copy(met[t][:], d_rows[t][:].indirect(n2_l[:]))

        def put(t):
            nc.vector.tensor_tensor(z_rows[t][:].indirect(n1_l[:]), own[t][:], met[t][:], ALU.add)

        for t in range(PACK - 1):
            leave(z_rows, y_bank, t)
        leave_together((d_rows, d_bank, 0), (z_rows, y_bank, 3))
        leave_together((d_rows, d_bank, 1), (d_rows, d_bank, 2), (d_rows, d_bank, 3))

        for t in range(PACK - 1):
            fetch_own(t)
        fetch_met(0)
        fetch_own(3)
        put(0)
        for t in range(1, PACK):
            fetch_met(t)
        for t in range(1, PACK):
            put(t)
        for t in range(PACK):
            for cols in halves:
                nc.scalar.copy(z_view[:, cols, t], z_rows[t][:, cols])

        d_codes = gather("d_codes", d_table, k1_l, U32, tag="d_rows3")
        z_codes = sb("z_codes", S, U32)
        z_plane = sb("z_plane", S, U8)

        def quantize_z(half):
            cols = halves[half]
            nc.vector.quantize_mx(out=z_codes[:, cols].bitcast(FP8X4), scales=z_plane[:, cols],
                                  in_=z_grouped[:, PACK * cols.start : PACK * cols.stop])

        quantize_z(0)
        d_codes_first = deal("d_codes_first", d_codes, slice(0, 1), U32, 4)
        quantize_z(1)
        d_codes_rest = deal("d_codes_rest", d_codes, slice(1, PACK), U32, 4, tag="z_grouped")
        zq = (z_codes, z_plane)

        gates = [sb(f"gates{t}", S, F32) for t in range(PACK)]
        st_rows = [sb(f"st_rows{t}", S, F32) for t in range(PACK)]
        other = [sb(f"other{t}", S, F32) for t in range(PACK)]
        out_view = out.rearrange("(p t) c -> p t c", t=PACK)

        def places(cols):
            return n3_l[:, cols.start // 16 : cols.stop // 16]

        h_rows = [sb(f"h_rows{t}", S, F32) for t in range(PACK)]

        def make_h(t):
            if t == 0:
                pieces = [(psum.tile([P, S], F32, name=f"h_first{half}", tag=f"bank{half}"), cols) for half, cols in enumerate(halves)]
                lhs, first = (d_codes_first, d_plane), 0
            else:
                pieces = [(psum.tile([P, S], F32, name=f"h_bank{t}", tag=f"bank{1 + t % 2}"), slice(0, S))]
                lhs, first = (d_codes_rest, d_plane), 1
            for bank, cols in pieces:
                product(bank, lhs, t, zq, cols, first)
                if t == 1:
                    nc.vector.tensor_scalar_mul(h_rows[t][:, cols], bank[:, cols], 0.0625)
                else:
                    nc.scalar.activation(h_rows[t][:, cols], bank[:, cols], ACT.Copy, scale=0.0625)
            return pieces

        h_pieces = {t: make_h(t) for t in range(2)}

        def gate(t):
            pieces = h_pieces[t] if t < 2 else make_h(t)
            for cols in halves:
                nc.scalar.activation(gates[t][:, cols], h_rows[t][:].indirect(places(cols)), ACT.Sigmoid)
            for bank, cols in pieces:
                nc.vector.scalar_tensor_tensor(st_rows[t][:, cols], bank[:, cols], 0.0625, gates[t][:, cols], ALU.mult, ALU.mult)

        gate(0)
        for t in range(PACK):
            last = t + 1 == PACK
            for cols in [halves[0], slice(256, 384), slice(384, 512)] if last else halves:
                nc.vector.tensor_copy(other[t][:, cols], st_rows[t][:].indirect(places(cols)))
            if not last:
                gate(t + 1)
            result = sb(f"result{t}", S, F32, tag=f"h_rows{(t + 1) % PACK}")
            for cols in [halves[0], slice(256, 384), slice(384, 512)] if last else [slice(0, S)]:
                nc.vector.tensor_tensor(result[:, cols], st_rows[t][:, cols], other[t][:, cols], ALU.max)
                nc.sync.dma_start(out_view[:, t, cols], result[:, cols])
